import numpy as np
import ml_dtypes


def mxq(x, axis, fmt="e4m3"):
    dtype, down = {"e4m3": (ml_dtypes.float8_e4m3fn, 7), "e5m2": (ml_dtypes.float8_e5m2, 14)}[fmt]
    v = np.moveaxis(np.asarray(x, np.float32).astype(ml_dtypes.bfloat16).astype(np.float64), axis, -1)
    blocks = v.reshape(v.shape[:-1] + (-1, 32))
    amax = np.abs(blocks).max(-1, keepdims=True)
    byte = np.maximum(np.where(amax > 0, np.frexp(amax)[1] - 1 + 127, 0) - down, 1)
    scale = np.exp2(byte - 127.0)
    codes = (blocks / scale).astype(np.float32).astype(dtype).astype(np.float64)
    return np.moveaxis((codes * scale).reshape(v.shape), -1, axis)


WIDE = False


def mx_kscale(k):
    if not WIDE:
        return np.ones(k)
    levels = np.array([10, -10, 5, -5, 0])
    if k % 512:
        return np.exp2(np.random.permutation(np.resize(levels, k // 32))).repeat(32)
    a = np.empty((k // 512, 16))
    for p in range(k // 512):
        a[p, :8] = np.random.permutation(np.resize(levels, 8))
        for g in range(8):
            far = levels[np.abs(levels - a[p, g]) >= 10]
            a[p, g + 8] = far[np.random.randint(len(far))]
    return np.exp2(a.ravel()).repeat(32)


def f64(x):
    return np.asarray(x).astype(np.float64)


def striped(idx):
    return np.tile(idx.reshape(-1, 16).T, (8, 1)).astype(np.uint16)


def unstriped(offs):
    return offs[:16].T.reshape(-1).astype(np.int64)


def striped8(idx):
    return np.concatenate([x.reshape(-1, 16).T for x in idx]).astype(np.uint16)


def runs(offs, k):
    lists = np.stack([offs[16 * r : 16 * r + 16].T.reshape(-1) for r in range(8)]).astype(np.int64)
    return lists[np.arange(k) % 512 // 64]


def pack_weight(w):
    k, n = w.shape
    w = f64(np.asarray(w, np.float32).astype(ml_dtypes.bfloat16)).reshape(k // 32, 32, n)
    amax = np.abs(w).max(1)
    byte = np.clip(np.where(amax > 0, np.frexp(amax)[1] - 1 + 127 - 7, 1), 1, 254)
    scaled = (w * np.exp2(127.0 - byte)[:, None, :]).reshape(k, n).astype(np.float32)
    words = np.ascontiguousarray(scaled.reshape(k // 512, 128, 4, n).transpose(0, 1, 3, 2)).astype(ml_dtypes.float8_e4m3fn).view(np.uint8)
    return words, np.ascontiguousarray(byte.astype(np.uint8).reshape(k // 512, 16, n))


def unpack_weight(words, scales):
    g, p, n, _ = words.shape
    vals = np.ascontiguousarray(words).view(ml_dtypes.float8_e4m3fn).astype(np.float64) * np.repeat(np.exp2(scales.astype(np.float64) - 127.0), 8, axis=1)[..., None]
    return vals.transpose(0, 1, 3, 2).reshape(g * 512, n)


K, T, S, H, C = 512, 2048, 512, 512, 512


def setup_inputs():
    n = np.random.standard_normal
    s = mx_kscale(K)[:, None]
    packed_xT = pack_weight(n((K, T)) * s)
    return {
        "x_words": packed_xT[0],
        "x_scales": packed_xT[1],
        "w1": (n((K, H)) / np.sqrt(K) / s).astype(np.float32),
        "w2": (n((K, H)) / np.sqrt(K) / s).astype(np.float32),
        "gs": (np.random.uniform(0.5, 1.5, (K, 1)) / s).astype(np.float32),
        "offs": striped(np.random.permutation(T)[:S]),
        "two": striped(np.random.permutation(T)[:S]),
        "n1": striped8(np.stack([np.random.permutation(S) for _ in range(8)])),
        "n2": striped8(np.stack([np.random.permutation(S) for _ in range(8)])),
        "cand": striped(np.random.permutation(T)[:C]),
        "n3": striped8(np.stack([np.random.permutation(S) for _ in range(8)])),
        "n4": striped8(np.stack([np.random.permutation(S) for _ in range(8)])),
    }


def reference(x_words, x_scales, w1, w2, gs, offs, two, n1, n2, cand, n3, n4):
    x_cand = unpack_weight(x_words, x_scales)[:, unstriped(cand)]
    xq = unpack_weight(x_words, x_scales)[:, unstriped(offs)]
    y = mxq(f64(w1), 0, "e4m3").T @ xq
    x_two = unpack_weight(x_words, x_scales)[:, unstriped(two)]
    d = mxq(f64(w2), 0, "e4m3").T @ x_two
    z = f64(gs) * (np.maximum(y, d[np.arange(H)[:, None], runs(n2, H)]) - (np.minimum(y[np.arange(H)[:, None], runs(n1, H)], d)))
    s = 0.0625 * ((x_cand.T @ mxq(z, 0, "e4m3")))
    return s[np.arange(C)[:, None], runs(n3, C)] + 0.75 * (s[np.arange(C)[:, None], runs(n4, C)])

@@ -1,0 +1,164 @@
+from contextlib import ExitStack
+
+import concourse.mybir as mybir
+
+K, T, S, H, C = 512, 2048, 512, 512, 512
+FLOPS = 2 * K * H * S * 2 + 2 * H * C * S
+
+F32 = mybir.dt.float32
+BF16 = mybir.dt.bfloat16
+I32 = mybir.dt.int32
+U32 = mybir.dt.uint32
+U16 = mybir.dt.uint16
+U8 = mybir.dt.uint8
+FP8X4 = mybir.dt.float8_e4m3fn_x4
+ALU = mybir.AluOpType
+COPY = mybir.ActivationFunctionType.Copy
+
+P = 128
+PACK = 4
+TILES = 4
+HALF = S // 2
+RUN = 8
+
+
+def tile_picked_twcmaxbsum_none_p_kernel(tc, x_words, x_scales, w1, w2, gs, offs, two, n1, n2, cand, n3, n4, out):
+    nc = tc.nc
+    with ExitStack() as ctx:
+        lists = ctx.enter_context(tc.tile_pool(name="lists", bufs=1))
+        keep = ctx.enter_context(tc.tile_pool(name="keep", bufs=1))
+        psum = ctx.enter_context(tc.psum_pool(name="psum", bufs=1))
+
+        def load_list(src, name):
+            tile = lists.tile([P, S // 16], U16, name=name)
+            nc.sync.dma_start(tile[:], src)
+            return tile
+
+        table_scales = keep.tile([P, T], U8, name="table_scales", align_bytes=64)
+        nc.vector.memset(table_scales[:].bitcast(I32), 0)
+        offs_sb = load_list(offs, "offs_sb")
+        for q in range(4):
+            nc.sync.dma_start(table_scales[32 * q : 32 * q + 4, :].bitcast(I32), x_scales[0, 4 * q : 4 * q + 4, :].bitcast(I32))
+        two_sb = load_list(two, "two_sb")
+        cand_sb = load_list(cand, "cand_sb")
+        w1_raw = keep.tile([P, PACK, H], F32, name="w1_raw")
+        nc.sync.dma_start(w1_raw[:], w1.rearrange("(p j) c -> p j c", j=PACK))
+        table_words = keep.tile([P, T], U32, name="table_words", align_bytes=64)
+        nc.sync.dma_start(table_words[:].bitcast(I32), x_words[0].rearrange("p n t -> p (n t)").bitcast(I32))
+        w2_raw = []
+        for c in range(2):
+            part = keep.tile([P, PACK, H // 2], F32, name="w2_raw%d" % c)
+            nc.sync.dma_start(part[:], w2.rearrange("(p j) c -> p j c", j=PACK)[:, :, c * (H // 2) : (c + 1) * (H // 2)])
+            w2_raw.append(part)
+        n1_sb = load_list(n1, "n1_sb")
+        n2_sb = load_list(n2, "n2_sb")
+        gs_sb = keep.tile([P, TILES], F32, name="gs_sb")
+        nc.sync.dma_start(gs_sb[:], gs.rearrange("(p t) o -> p (t o)", t=TILES))
+        n4_sb = load_list(n4, "n4_sb")
+        n3_sb = load_list(n3, "n3_sb")
+
+        def gather_scales(list_sb, name):
+            picked = keep.tile([P, S], U8, name=name, align_bytes=64)
+            nc.vector.tensor_copy(picked[:], table_scales[:].indirect(list_sb[:]))
+            return picked
+
+        def gather_words(list_sb, name, tag):
+            picked = keep.tile([P, S], U32, name=name, tag=tag, align_bytes=64)
+            nc.vector.tensor_copy(picked[:], table_words[:].indirect(list_sb[:]))
+            return picked
+
+        def round_weights(grouped, raw, first, count):
+            nc.scalar.activation(
+                grouped[:].rearrange("p (t m j) -> p m j t", t=TILES, j=PACK)[:, first : first + count],
+                raw[:].rearrange("p j (m t) -> p m j t", t=TILES),
+                COPY,
+            )
+
+        def quantize(grouped, width, name):
+            codes = keep.tile([P, width], U32, name=name + "_codes", align_bytes=64)
+            scales = keep.tile([P, width], U8, name=name + "_scales", align_bytes=64)
+            nc.vector.quantize_mx(out=codes[:].bitcast(FP8X4), scales=scales[:], in_=grouped)
+            return codes, scales
+
+        def product(bank, left, left_scales, t, right, right_scales):
+            cols = slice(t * P, (t + 1) * P)
+            nc.tensor.matmul_mx(out=bank, lhsT=left[:, cols].bitcast(FP8X4), lhsT_scale=left_scales[:, cols],
+                                rhs=right[:].bitcast(FP8X4), rhs_scale=right_scales[:], start=True, stop=True)
+
+        xq_scales = gather_scales(offs_sb, "xq_scales")
+        two_scales = gather_scales(two_sb, "two_scales")
+        cand_listed = gather_scales(cand_sb, "cand_listed")
+        w1_grouped = keep.tile([P, H * PACK], BF16, name="w1_grouped", tag="w1_grouped", align_bytes=64)
+        round_weights(w1_grouped, w1_raw, 0, P)
+        xq_words = gather_words(offs_sb, "xq_words", "xq_words")
+        w1_codes, w1_scales = quantize(w1_grouped[:], H, "w1")
+        two_words = gather_words(two_sb, "two_words", "w1_grouped")
+        w2_grouped = keep.tile([P, H * PACK], BF16, name="w2_grouped", align_bytes=64)
+        for c in range(2):
+            round_weights(w2_grouped, w2_raw[c], c * (P // 2), P // 2)
+        cand_scales = keep.tile([P, C], U8, name="cand_scales", align_bytes=64)
+        nc.vector.tensor_copy(
+            cand_scales[:].bitcast(I32).rearrange("p (t a b) -> p t a b", t=TILES, b=RUN // 4),
+            cand_listed[:].bitcast(I32).rearrange("p (a t b) -> p t a b", t=TILES, b=RUN // 4),
+        )
+        w2_codes, w2_scales = quantize(w2_grouped[:], H, "w2")
+
+        y_bank, d_bank, y_sb, d_sb = [], [], [], []
+        for t in range(TILES):
+            yb = psum.tile([P, S], F32, name="y_bank%d" % t, tag="bank%d" % (2 * t))
+            product(yb[:], w1_codes, w1_scales, t, xq_words, xq_scales)
+            ys = keep.tile([P, S], F32, name="y_sb%d" % t)
+            nc.scalar.copy(ys[:], yb[:])
+            db = psum.tile([P, S], F32, name="d_bank%d" % t, tag="bank%d" % (2 * t + 1))
+            product(db[:], w2_codes, w2_scales, t, two_words, two_scales)
+            ds = keep.tile([P, S], F32, name="d_sb%d" % t)
+            nc.scalar.copy(ds[:], db[:])
+            y_bank.append(yb)
+            d_bank.append(db)
+            y_sb.append(ys)
+            d_sb.append(ds)
+
+        s_sb = [keep.tile([P, 2 * S], F32, name="s_sb%d" % t) for t in range(TILES)]
+        z_codes, z_scales = [], []
+        for h in range(2):
+            cols = slice(h * HALF, (h + 1) * HALF)
+            entries = slice(h * HALF // 16, (h + 1) * HALF // 16)
+            z_grouped = keep.tile([P, HALF, PACK], BF16, name="z_grouped%d" % h, align_bytes=64)
+            for t in range(TILES):
+                y_far = keep.tile([P, HALF], F32, name="y_far%d_%d" % (h, t))
+                nc.vector.tensor_copy(y_far[:], y_sb[t][:].indirect(n1_sb[:, entries]))
+                d_far = keep.tile([P, HALF], F32, name="d_far%d_%d" % (h, t), tag="d_far%d_%d" % (h, t), align_bytes=64)
+                nc.vector.tensor_copy(d_far[:], d_sb[t][:].indirect(n2_sb[:, entries]))
+                smaller = keep.tile([P, HALF], F32, name="smaller%d_%d" % (h, t))
+                nc.vector.tensor_tensor(smaller[:], y_far[:], d_bank[t][:, cols], ALU.min)
+                larger = s_sb[t][:, S + h * HALF : S + (h + 1) * HALF]
+                nc.vector.tensor_tensor(larger, d_far[:], y_bank[t][:, cols], ALU.max)
+                spread = keep.tile([P, HALF], F32, name="spread%d_%d" % (h, t))
+                nc.gpsimd.tensor_tensor(spread[:], larger, smaller[:], ALU.subtract)
+                nc.scalar.activation(z_grouped[:, :, t], spread[:], COPY, scale=gs_sb[:, t : t + 1])
+            if h == 1:
+                cand_words = keep.tile([P, C], U32, name="cand_words", tag="d_far1_3", align_bytes=64)
+                nc.vector.tensor_copy(cand_words[:].rearrange("p (t a b) -> p a t b", t=TILES, b=RUN), table_words[:].indirect(cand_sb[:]))
+            codes, scales = quantize(z_grouped[:].rearrange("p c t -> p (c t)"), HALF, "z%d" % h)
+            z_codes.append(codes)
+            z_scales.append(scales)
+
+        s_bank = [psum.tile([P, S], F32, name="s_bank%d" % t, tag="bank%d" % t) for t in range(TILES)]
+        for h in range(2):
+            cols = slice(h * HALF, (h + 1) * HALF)
+            for t in range(TILES):
+                product(s_bank[t][:, cols], cand_words, cand_scales, t, z_codes[h], z_scales[h])
+                nc.scalar.activation(s_sb[t][:, cols], s_bank[t][:, cols], COPY, scale=0.0625)
+
+        out_rows = out.rearrange("(a t b) n -> t a b n", t=TILES, b=RUN)
+        for t in range(TILES):
+            far4 = keep.tile([P, S], F32, name="far4_%d" % t)
+            nc.vector.tensor_scalar(far4[:], s_sb[t][:].indirect(n4_sb[:]), 0.75, 0.0, ALU.mult, ALU.add)
+            result = keep.tile([P, S], F32, name="result%d" % t)
+            if t < TILES - 1:
+                far3 = keep.tile([P, S], F32, name="far3_%d" % t)
+                nc.vector.tensor_copy(far3[:], s_sb[t][:].indirect(n3_sb[:]))
+                nc.gpsimd.tensor_tensor(result[:], far3[:], far4[:], ALU.add)
+            else:
+                nc.vector.tensor_tensor(result[:], s_sb[t][:].indirect(n3_sb[:]), far4[:], ALU.add)
+            nc.sync.dma_start(out_rows[t], result[:])

@@ -13,6 +13,7 @@ U16 = mybir.dt.uint16
 U8 = mybir.dt.uint8
 FP8X4 = mybir.dt.float8_e4m3fn_x4
 ALU = mybir.AluOpType
+RELU = mybir.ActivationFunctionType.Relu
 COPY = mybir.ActivationFunctionType.Copy
 
 P = 128
@@ -27,6 +28,7 @@ def tile_picked_twcmaxbsum_none_p_kernel(tc, x_words, x_scales, w1, w2, gs, offs
     with ExitStack() as ctx:
         lists = ctx.enter_context(tc.tile_pool(name="lists", bufs=1))
         keep = ctx.enter_context(tc.tile_pool(name="keep", bufs=1))
+        ring = ctx.enter_context(tc.tile_pool(name="ring", bufs=2))
         psum = ctx.enter_context(tc.psum_pool(name="psum", bufs=1))
 
         def load_list(src, name):
@@ -35,16 +37,20 @@ def tile_picked_twcmaxbsum_none_p_kernel(tc, x_words, x_scales, w1, w2, gs, offs
             return tile
 
         table_scales = keep.tile([P, T], U8, name="table_scales", align_bytes=64)
-        nc.vector.memset(table_scales[:].bitcast(I32), 0)
+        nc.vector.memset(table_scales[:, : T // 2].bitcast(I32), 0)
+        nc.gpsimd.memset(table_scales[:, T // 2 :].bitcast(I32), 0)
         offs_sb = load_list(offs, "offs_sb")
-        for q in range(4):
-            nc.sync.dma_start(table_scales[32 * q : 32 * q + 4, :].bitcast(I32), x_scales[0, 4 * q : 4 * q + 4, :].bitcast(I32))
+        for r in range(4):
+            (nc.sync if r % 2 == 0 else nc.scalar).dma_start(table_scales[r:P:32, :].bitcast(I32), x_scales[0, r:16:4, :].bitcast(I32))
         two_sb = load_list(two, "two_sb")
         cand_sb = load_list(cand, "cand_sb")
-        w1_raw = keep.tile([P, PACK, H], F32, name="w1_raw")
-        nc.sync.dma_start(w1_raw[:], w1.rearrange("(p j) c -> p j c", j=PACK))
         table_words = keep.tile([P, T], U32, name="table_words", align_bytes=64)
         nc.sync.dma_start(table_words[:].bitcast(I32), x_words[0].rearrange("p n t -> p (n t)").bitcast(I32))
+        w1_raw = []
+        for c in range(2):
+            part = keep.tile([P, PACK, H // 2], F32, name="w1_raw%d" % c, tag="w1_raw%d" % c, align_bytes=64)
+            nc.sync.dma_start(part[:], w1.rearrange("(p j) c -> p j c", j=PACK)[:, :, c * (H // 2) : (c + 1) * (H // 2)])
+            w1_raw.append(part)
         w2_raw = []
         for c in range(2):
             part = keep.tile([P, PACK, H // 2], F32, name="w2_raw%d" % c)
@@ -58,7 +64,7 @@ def tile_picked_twcmaxbsum_none_p_kernel(tc, x_words, x_scales, w1, w2, gs, offs
         n3_sb = load_list(n3, "n3_sb")
 
         def gather_scales(list_sb, name):
-            picked = keep.tile([P, S], U8, name=name, align_bytes=64)
+            picked = keep.tile([P, S], U8, name=name, tag=name, align_bytes=64)
             nc.vector.tensor_copy(picked[:], table_scales[:].indirect(list_sb[:]))
             return picked
 
@@ -67,98 +73,145 @@ def tile_picked_twcmaxbsum_none_p_kernel(tc, x_words, x_scales, w1, w2, gs, offs
             nc.vector.tensor_copy(picked[:], table_words[:].indirect(list_sb[:]))
             return picked
 
-        def round_weights(grouped, raw, first, count):
-            nc.scalar.activation(
-                grouped[:].rearrange("p (t m j) -> p m j t", t=TILES, j=PACK)[:, first : first + count],
-                raw[:].rearrange("p j (m t) -> p m j t", t=TILES),
-                COPY,
-            )
+        def round_weights(grouped, raw, half, first, count, on_scalar):
+            dealt = grouped[:].rearrange("p (t m j) -> p m j t", t=TILES, j=PACK)[:, half * (P // 2) + first : half * (P // 2) + first + count]
+            rows = raw[half][:].rearrange("p j (m t) -> p m j t", t=TILES)[:, first : first + count]
+            if on_scalar:
+                nc.scalar.activation(dealt, rows, COPY)
+            else:
+                nc.vector.tensor_copy(dealt, rows)
 
-        def quantize(grouped, width, name):
-            codes = keep.tile([P, width], U32, name=name + "_codes", align_bytes=64)
-            scales = keep.tile([P, width], U8, name=name + "_scales", align_bytes=64)
-            nc.vector.quantize_mx(out=codes[:].bitcast(FP8X4), scales=scales[:], in_=grouped)
+        def planes(name, tag):
+            codes = keep.tile([P, S], U32, name=name + "_codes", tag=tag, align_bytes=64)
+            scales = keep.tile([P, S], U8, name=name + "_scales", align_bytes=64)
             return codes, scales
 
-        def product(bank, left, left_scales, t, right, right_scales):
-            cols = slice(t * P, (t + 1) * P)
-            nc.tensor.matmul_mx(out=bank, lhsT=left[:, cols].bitcast(FP8X4), lhsT_scale=left_scales[:, cols],
-                                rhs=right[:].bitcast(FP8X4), rhs_scale=right_scales[:], start=True, stop=True)
+        def quantize(codes, scales, grouped, first, count):
+            nc.vector.quantize_mx(
+                out=codes[:, first : first + count].bitcast(FP8X4),
+                scales=scales[:, first : first + count],
+                in_=grouped[:, PACK * first : PACK * (first + count)],
+            )
+
+        def product(bank, left, left_scales, t, right, right_scales, cols):
+            rows = slice(t * P, (t + 1) * P)
+            nc.tensor.matmul_mx(out=bank, lhsT=left[:, rows].bitcast(FP8X4), lhsT_scale=left_scales[:, rows],
+                                rhs=right[:, cols].bitcast(FP8X4), rhs_scale=right_scales[:, cols], start=True, stop=True)
 
         xq_scales = gather_scales(offs_sb, "xq_scales")
         two_scales = gather_scales(two_sb, "two_scales")
         cand_listed = gather_scales(cand_sb, "cand_listed")
-        w1_grouped = keep.tile([P, H * PACK], BF16, name="w1_grouped", tag="w1_grouped", align_bytes=64)
-        round_weights(w1_grouped, w1_raw, 0, P)
         xq_words = gather_words(offs_sb, "xq_words", "xq_words")
-        w1_codes, w1_scales = quantize(w1_grouped[:], H, "w1")
-        two_words = gather_words(two_sb, "two_words", "w1_grouped")
-        w2_grouped = keep.tile([P, H * PACK], BF16, name="w2_grouped", align_bytes=64)
-        for c in range(2):
-            round_weights(w2_grouped, w2_raw[c], c * (P // 2), P // 2)
-        cand_scales = keep.tile([P, C], U8, name="cand_scales", align_bytes=64)
+        w1_grouped = keep.tile([P, H * PACK], BF16, name="w1_grouped", tag="grouped", align_bytes=64)
+        round_weights(w1_grouped, w1_raw, 0, 0, P // 2, True)
+        round_weights(w1_grouped, w1_raw, 1, 0, P // 4, True)
+        round_weights(w1_grouped, w1_raw, 1, P // 4, P // 4, False)
+        w1_codes, w1_scales = planes("w1", "w1_codes")
+        quantize(w1_codes, w1_scales, w1_grouped, 0, P)
+        cand_scales = keep.tile([P, C], U8, name="cand_scales", tag="w1_raw1", align_bytes=64)
         nc.vector.tensor_copy(
             cand_scales[:].bitcast(I32).rearrange("p (t a b) -> p t a b", t=TILES, b=RUN // 4),
             cand_listed[:].bitcast(I32).rearrange("p (a t b) -> p t a b", t=TILES, b=RUN // 4),
         )
-        w2_codes, w2_scales = quantize(w2_grouped[:], H, "w2")
+        quantize(w1_codes, w1_scales, w1_grouped, P, P)
+        quantize(w1_codes, w1_scales, w1_grouped, 2 * P, 2 * P)
+        two_words = gather_words(two_sb, "two_words", "cand_listed")
+        w2_grouped = keep.tile([P, H * PACK], BF16, name="w2_grouped", align_bytes=64)
+        round_weights(w2_grouped, w2_raw, 0, 0, P // 2, True)
 
+        halves = [slice(0, HALF), slice(HALF, S)]
+        whole = slice(0, S)
         y_bank, d_bank, y_sb, d_sb = [], [], [], []
         for t in range(TILES):
             yb = psum.tile([P, S], F32, name="y_bank%d" % t, tag="bank%d" % (2 * t))
-            product(yb[:], w1_codes, w1_scales, t, xq_words, xq_scales)
-            ys = keep.tile([P, S], F32, name="y_sb%d" % t)
+            ys = keep.tile([P, S], F32, name="y_sb%d" % t, tag="y_sb%d" % t, align_bytes=64)
+            product(yb[:], w1_codes, w1_scales, t, xq_words, xq_scales, whole)
             nc.scalar.copy(ys[:], yb[:])
+            if t == 0:
+                round_weights(w2_grouped, w2_raw, 1, 0, P // 2, True)
+            y_bank.append(yb)
+            y_sb.append(ys)
+        y_far = [keep.tile([P, S], F32, name="y_far%d" % t) for t in range(TILES)]
+
+        def fetch_y(t):
+            for cols in halves:
+                nc.vector.tensor_copy(y_far[t][:, cols], y_sb[t][:].indirect(n1_sb[:, cols.start // 16 : cols.stop // 16]))
+
+        fetch_y(0)
+        w2_codes, w2_scales = planes("w2", "y_sb0")
+        quantize(w2_codes, w2_scales, w2_grouped, 0, H)
+        for t in range(1, TILES):
+            fetch_y(t)
+        for t in range(TILES):
             db = psum.tile([P, S], F32, name="d_bank%d" % t, tag="bank%d" % (2 * t + 1))
-            product(db[:], w2_codes, w2_scales, t, two_words, two_scales)
+            product(db[:], w2_codes, w2_scales, t, two_words, two_scales, whole)
             ds = keep.tile([P, S], F32, name="d_sb%d" % t)
             nc.scalar.copy(ds[:], db[:])
-            y_bank.append(yb)
             d_bank.append(db)
-            y_sb.append(ys)
             d_sb.append(ds)
 
         s_sb = [keep.tile([P, 2 * S], F32, name="s_sb%d" % t) for t in range(TILES)]
-        z_codes, z_scales = [], []
-        for h in range(2):
-            cols = slice(h * HALF, (h + 1) * HALF)
-            entries = slice(h * HALF // 16, (h + 1) * HALF // 16)
-            z_grouped = keep.tile([P, HALF, PACK], BF16, name="z_grouped%d" % h, align_bytes=64)
-            for t in range(TILES):
-                y_far = keep.tile([P, HALF], F32, name="y_far%d_%d" % (h, t))
-                nc.vector.tensor_copy(y_far[:], y_sb[t][:].indirect(n1_sb[:, entries]))
-                d_far = keep.tile([P, HALF], F32, name="d_far%d_%d" % (h, t), tag="d_far%d_%d" % (h, t), align_bytes=64)
-                nc.vector.tensor_copy(d_far[:], d_sb[t][:].indirect(n2_sb[:, entries]))
-                smaller = keep.tile([P, HALF], F32, name="smaller%d_%d" % (h, t))
-                nc.vector.tensor_tensor(smaller[:], y_far[:], d_bank[t][:, cols], ALU.min)
-                larger = s_sb[t][:, S + h * HALF : S + (h + 1) * HALF]
-                nc.vector.tensor_tensor(larger, d_far[:], y_bank[t][:, cols], ALU.max)
-                spread = keep.tile([P, HALF], F32, name="spread%d_%d" % (h, t))
-                nc.gpsimd.tensor_tensor(spread[:], larger, smaller[:], ALU.subtract)
-                nc.scalar.activation(z_grouped[:, :, t], spread[:], COPY, scale=gs_sb[:, t : t + 1])
-            if h == 1:
-                cand_words = keep.tile([P, C], U32, name="cand_words", tag="d_far1_3", align_bytes=64)
-                nc.vector.tensor_copy(cand_words[:].rearrange("p (t a b) -> p a t b", t=TILES, b=RUN), table_words[:].indirect(cand_sb[:]))
-            codes, scales = quantize(z_grouped[:].rearrange("p c t -> p (c t)"), HALF, "z%d" % h)
-            z_codes.append(codes)
-            z_scales.append(scales)
+        z_codes, z_scales = planes("z", "z_codes")
+        z_grouped = keep.tile([P, S * PACK], BF16, name="z_grouped", align_bytes=64)
+        z_slots = z_grouped[:].rearrange("p (c t) -> p c t", t=PACK)
 
-        s_bank = [psum.tile([P, S], F32, name="s_bank%d" % t, tag="bank%d" % t) for t in range(TILES)]
-        for h in range(2):
-            cols = slice(h * HALF, (h + 1) * HALF)
-            for t in range(TILES):
-                product(s_bank[t][:, cols], cand_words, cand_scales, t, z_codes[h], z_scales[h])
-                nc.scalar.activation(s_sb[t][:, cols], s_bank[t][:, cols], COPY, scale=0.0625)
+        excess = keep.tile([P, S], F32, name="excess")
+        nc.gpsimd.tensor_tensor(excess[:], d_sb[0][:], y_far[0][:], ALU.subtract)
+        clipped = keep.tile([P, S], F32, name="clipped")
+        nc.scalar.activation(clipped[:], excess[:], RELU)
+        smaller0 = keep.tile([P, S], F32, name="smaller0")
+        nc.gpsimd.tensor_tensor(smaller0[:], d_sb[0][:], clipped[:], ALU.subtract)
+
+        def spread_piece(t, first, count):
+            cols = slice(first, first + count)
+            entries = slice(first // 16, (first + count) // 16)
+            name = "%d_%d" % (t, first)
+            d_far = ring.tile([P, count], F32, name="d_far" + name, tag="fetched", align_bytes=64)
+            nc.vector.tensor_copy(d_far[:], d_sb[t][:].indirect(n2_sb[:, entries]))
+            if t == 0:
+                smaller = smaller0[:, cols]
+            else:
+                piece = keep.tile([P, count], F32, name="smaller" + name)
+                smaller = piece[:]
+                nc.vector.tensor_tensor(smaller, y_far[t][:, cols], d_bank[t][:, cols], ALU.min)
+            larger = s_sb[t][:, S + first : S + first + count]
+            nc.vector.tensor_tensor(larger, d_far[:], y_bank[t][:, cols], ALU.max)
+            spread = keep.tile([P, count], F32, name="spread" + name)
+            nc.gpsimd.tensor_tensor(spread[:], larger, smaller, ALU.subtract)
+            nc.scalar.activation(z_slots[:, cols, t], spread[:], COPY, scale=gs_sb[:, t : t + 1])
+
+        for t in (1, 0, 2):
+            spread_piece(t, 0, HALF)
+            spread_piece(t, HALF, HALF)
+        spread_piece(3, 0, HALF)
+        spread_piece(3, HALF, P)
+        spread_piece(3, HALF + P, P)
+        cand_words = ring.tile([P, C], U32, name="cand_words", tag="fetched", align_bytes=64)
+        nc.vector.tensor_copy(cand_words[:].rearrange("p (t a b) -> p a t b", t=TILES, b=RUN), table_words[:].indirect(cand_sb[:]))
+        quantize(z_codes, z_scales, z_grouped, 0, HALF)
+        quantize(z_codes, z_scales, z_grouped, HALF, HALF)
+
+        bank = 0
+        for t in range(TILES):
+            for cols in halves if t == 0 else [whole]:
+                s_bank = psum.tile([P, cols.stop - cols.start], F32, name="s_bank%d" % bank, tag="bank%d" % bank)
+                product(s_bank[:], cand_words, cand_scales, t, z_codes, z_scales, cols)
+                nc.scalar.activation(s_sb[t][:, cols], s_bank[:], COPY, scale=0.0625)
+                bank = bank + 1
 
         out_rows = out.rearrange("(a t b) n -> t a b n", t=TILES, b=RUN)
         for t in range(TILES):
-            far4 = keep.tile([P, S], F32, name="far4_%d" % t)
-            nc.vector.tensor_scalar(far4[:], s_sb[t][:].indirect(n4_sb[:]), 0.75, 0.0, ALU.mult, ALU.add)
-            result = keep.tile([P, S], F32, name="result%d" % t)
-            if t < TILES - 1:
-                far3 = keep.tile([P, S], F32, name="far3_%d" % t)
-                nc.vector.tensor_copy(far3[:], s_sb[t][:].indirect(n3_sb[:]))
-                nc.gpsimd.tensor_tensor(result[:], far3[:], far4[:], ALU.add)
-            else:
-                nc.vector.tensor_tensor(result[:], s_sb[t][:].indirect(n3_sb[:]), far4[:], ALU.add)
-            nc.sync.dma_start(out_rows[t], result[:])
+            for cols in halves if t == TILES - 1 else [whole]:
+                count = cols.stop - cols.start
+                entries = slice(cols.start // 16, cols.stop // 16)
+                name = "%d_%d" % (t, cols.start)
+                far4 = keep.tile([P, count], F32, name="far4_" + name)
+                nc.vector.tensor_scalar(far4[:], s_sb[t][:].indirect(n4_sb[:, entries]), 0.75, 0.0, ALU.mult, ALU.add)
+                result = keep.tile([P, count], F32, name="result" + name)
+                if t < TILES - 1 or cols.start == 0:
+                    far3 = keep.tile([P, count], F32, name="far3_" + name)
+                    nc.vector.tensor_copy(far3[:], s_sb[t][:].indirect(n3_sb[:, entries]))
+                    nc.gpsimd.tensor_tensor(result[:], far3[:], far4[:], ALU.add)
+                else:
+                    nc.vector.tensor_tensor(result[:], s_sb[t][:].indirect(n3_sb[:, entries]), far4[:], ALU.add)
+                nc.sync.dma_start(out_rows[t][:, :, cols], result[:])

@@ -13,18 +13,24 @@ U16 = mybir.dt.uint16
 U8 = mybir.dt.uint8
 FP8X4 = mybir.dt.float8_e4m3fn_x4
 ALU = mybir.AluOpType
-RELU = mybir.ActivationFunctionType.Relu
 COPY = mybir.ActivationFunctionType.Copy
+RELU = mybir.ActivationFunctionType.Relu
 
 P = 128
 PACK = 4
 TILES = 4
 HALF = S // 2
+GROUP = 16
 RUN = 8
+RELU_TILES = 2
+MX_ALIGN = 64
 
 
 def tile_picked_twcmaxbsum_none_p_kernel(tc, x_words, x_scales, w1, w2, gs, offs, two, n1, n2, cand, n3, n4, out):
     nc = tc.nc
+    halves = [slice(0, HALF), slice(HALF, S)]
+    whole = slice(0, S)
+
     with ExitStack() as ctx:
         lists = ctx.enter_context(tc.tile_pool(name="lists", bufs=1))
         keep = ctx.enter_context(tc.tile_pool(name="keep", bufs=1))
@@ -32,30 +38,36 @@ def tile_picked_twcmaxbsum_none_p_kernel(tc, x_words, x_scales, w1, w2, gs, offs
         psum = ctx.enter_context(tc.psum_pool(name="psum", bufs=1))
 
         def load_list(src, name):
-            tile = lists.tile([P, S // 16], U16, name=name)
+            tile = lists.tile([P, S // GROUP], U16, name=name)
             nc.sync.dma_start(tile[:], src)
             return tile
 
-        table_scales = keep.tile([P, T], U8, name="table_scales", align_bytes=64)
-        nc.vector.memset(table_scales[:, : T // 2].bitcast(I32), 0)
-        nc.gpsimd.memset(table_scales[:, T // 2 :].bitcast(I32), 0)
+        def entries(list_sb, cols):
+            return list_sb[:, cols.start // GROUP : cols.stop // GROUP]
+
+        def load_weights(w, name):
+            parts = []
+            for half in range(2):
+                part = keep.tile([P, PACK * H // 2], F32, name="%s%d" % (name, half), tag="%s%d" % (name, half), align_bytes=MX_ALIGN)
+                nc.sync.dma_start(
+                    part[:].rearrange("p (j c) -> p j c", j=PACK),
+                    w.rearrange("(p j) c -> p j c", j=PACK)[:, :, half * (H // 2) : (half + 1) * (H // 2)],
+                )
+                parts.append(part)
+            return parts
+
+        table_scales = keep.tile([P, T], U8, name="table_scales", align_bytes=MX_ALIGN)
+        nc.vector.memset(table_scales[:].bitcast(I32), 0)
         offs_sb = load_list(offs, "offs_sb")
         for r in range(4):
-            (nc.sync if r % 2 == 0 else nc.scalar).dma_start(table_scales[r:P:32, :].bitcast(I32), x_scales[0, r:16:4, :].bitcast(I32))
+            queue = nc.sync if r % 2 == 0 else nc.scalar
+            queue.dma_start(table_scales[r:P:32, :].bitcast(I32), x_scales[0, r:16:4, :].bitcast(I32))
         two_sb = load_list(two, "two_sb")
         cand_sb = load_list(cand, "cand_sb")
-        table_words = keep.tile([P, T], U32, name="table_words", align_bytes=64)
+        table_words = keep.tile([P, T], U32, name="table_words", align_bytes=MX_ALIGN)
         nc.sync.dma_start(table_words[:].bitcast(I32), x_words[0].rearrange("p n t -> p (n t)").bitcast(I32))
-        w1_raw = []
-        for c in range(2):
-            part = keep.tile([P, PACK, H // 2], F32, name="w1_raw%d" % c, tag="w1_raw%d" % c, align_bytes=64)
-            nc.sync.dma_start(part[:], w1.rearrange("(p j) c -> p j c", j=PACK)[:, :, c * (H // 2) : (c + 1) * (H // 2)])
-            w1_raw.append(part)
-        w2_raw = []
-        for c in range(2):
-            part = keep.tile([P, PACK, H // 2], F32, name="w2_raw%d" % c)
-            nc.sync.dma_start(part[:], w2.rearrange("(p j) c -> p j c", j=PACK)[:, :, c * (H // 2) : (c + 1) * (H // 2)])
-            w2_raw.append(part)
+        w1_raw = load_weights(w1, "w1_raw")
+        w2_raw = load_weights(w2, "w2_raw")
         n1_sb = load_list(n1, "n1_sb")
         n2_sb = load_list(n2, "n2_sb")
         gs_sb = keep.tile([P, TILES], F32, name="gs_sb")
@@ -64,26 +76,30 @@ def tile_picked_twcmaxbsum_none_p_kernel(tc, x_words, x_scales, w1, w2, gs, offs
         n3_sb = load_list(n3, "n3_sb")
 
         def gather_scales(list_sb, name):
-            picked = keep.tile([P, S], U8, name=name, tag=name, align_bytes=64)
+            picked = keep.tile([P, S], U8, name=name, tag=name, align_bytes=MX_ALIGN)
             nc.vector.tensor_copy(picked[:], table_scales[:].indirect(list_sb[:]))
             return picked
 
         def gather_words(list_sb, name, tag):
-            picked = keep.tile([P, S], U32, name=name, tag=tag, align_bytes=64)
+            picked = keep.tile([P, S], U32, name=name, tag=tag, align_bytes=MX_ALIGN)
             nc.vector.tensor_copy(picked[:], table_words[:].indirect(list_sb[:]))
             return picked
 
-        def round_weights(grouped, raw, half, first, count, on_scalar):
-            dealt = grouped[:].rearrange("p (t m j) -> p m j t", t=TILES, j=PACK)[:, half * (P // 2) + first : half * (P // 2) + first + count]
-            rows = raw[half][:].rearrange("p j (m t) -> p m j t", t=TILES)[:, first : first + count]
-            if on_scalar:
-                nc.scalar.activation(dealt, rows, COPY)
-            else:
-                nc.vector.tensor_copy(dealt, rows)
+        def dealt_views(grouped, raw, half, first, count):
+            start = half * (P // 2) + first
+            dealt = grouped[:].rearrange("p (t m j) -> p m j t", t=TILES, j=PACK)[:, start : start + count]
+            rows = raw[half][:].rearrange("p (j m t) -> p m j t", j=PACK, t=TILES)[:, first : first + count]
+            return dealt, rows
 
-        def planes(name, tag):
-            codes = keep.tile([P, S], U32, name=name + "_codes", tag=tag, align_bytes=64)
-            scales = keep.tile([P, S], U8, name=name + "_scales", align_bytes=64)
+        def round_on_scalar(*piece):
+            nc.scalar.activation(*dealt_views(*piece), COPY)
+
+        def round_on_vector(*piece):
+            nc.vector.tensor_copy(*dealt_views(*piece))
+
+        def mx_operand(name, tag):
+            codes = keep.tile([P, S], U32, name=name + "_codes", tag=tag, align_bytes=MX_ALIGN)
+            scales = keep.tile([P, S], U8, name=name + "_scales", align_bytes=MX_ALIGN)
             return codes, scales
 
         def quantize(codes, scales, grouped, first, count):
@@ -93,125 +109,139 @@ def tile_picked_twcmaxbsum_none_p_kernel(tc, x_words, x_scales, w1, w2, gs, offs
                 in_=grouped[:, PACK * first : PACK * (first + count)],
             )
 
+        def quantize_weights(codes, scales, grouped):
+            for first, count in ((0, P), (P, P), (2 * P, 2 * P)):
+                quantize(codes, scales, grouped, first, count)
+
         def product(bank, left, left_scales, t, right, right_scales, cols):
             rows = slice(t * P, (t + 1) * P)
-            nc.tensor.matmul_mx(out=bank, lhsT=left[:, rows].bitcast(FP8X4), lhsT_scale=left_scales[:, rows],
-                                rhs=right[:, cols].bitcast(FP8X4), rhs_scale=right_scales[:, cols], start=True, stop=True)
+            nc.tensor.matmul_mx(
+                out=bank,
+                lhsT=left[:, rows].bitcast(FP8X4),
+                lhsT_scale=left_scales[:, rows],
+                rhs=right[:, cols].bitcast(FP8X4),
+                rhs_scale=right_scales[:, cols],
+                start=True,
+                stop=True,
+            )
 
         xq_scales = gather_scales(offs_sb, "xq_scales")
         two_scales = gather_scales(two_sb, "two_scales")
         cand_listed = gather_scales(cand_sb, "cand_listed")
         xq_words = gather_words(offs_sb, "xq_words", "xq_words")
-        w1_grouped = keep.tile([P, H * PACK], BF16, name="w1_grouped", tag="grouped", align_bytes=64)
-        round_weights(w1_grouped, w1_raw, 0, 0, P // 2, True)
-        round_weights(w1_grouped, w1_raw, 1, 0, P // 4, True)
-        round_weights(w1_grouped, w1_raw, 1, P // 4, P // 4, False)
-        w1_codes, w1_scales = planes("w1", "w1_codes")
-        quantize(w1_codes, w1_scales, w1_grouped, 0, P)
-        cand_scales = keep.tile([P, C], U8, name="cand_scales", tag="w1_raw1", align_bytes=64)
+        w1_grouped = keep.tile([P, H * PACK], BF16, name="w1_grouped", tag="w1_grouped", align_bytes=MX_ALIGN)
+        round_on_scalar(w1_grouped, w1_raw, 0, 0, P // 2)
+        round_on_scalar(w1_grouped, w1_raw, 1, 0, P // 4)
+        round_on_vector(w1_grouped, w1_raw, 1, P // 4, P // 4)
+        w1_codes, w1_scales = mx_operand("w1", "w1_codes")
+        quantize_weights(w1_codes, w1_scales, w1_grouped)
+
+        cand_scales = keep.tile([P, C], U8, name="cand_scales", tag="w1_grouped", align_bytes=MX_ALIGN)
         nc.vector.tensor_copy(
             cand_scales[:].bitcast(I32).rearrange("p (t a b) -> p t a b", t=TILES, b=RUN // 4),
             cand_listed[:].bitcast(I32).rearrange("p (a t b) -> p t a b", t=TILES, b=RUN // 4),
         )
-        quantize(w1_codes, w1_scales, w1_grouped, P, P)
-        quantize(w1_codes, w1_scales, w1_grouped, 2 * P, 2 * P)
         two_words = gather_words(two_sb, "two_words", "cand_listed")
-        w2_grouped = keep.tile([P, H * PACK], BF16, name="w2_grouped", align_bytes=64)
-        round_weights(w2_grouped, w2_raw, 0, 0, P // 2, True)
+        w2_grouped = keep.tile([P, H * PACK], BF16, name="w2_grouped", align_bytes=MX_ALIGN)
+        round_on_scalar(w2_grouped, w2_raw, 0, 0, P // 2)
 
-        halves = [slice(0, HALF), slice(HALF, S)]
-        whole = slice(0, S)
-        y_bank, d_bank, y_sb, d_sb = [], [], [], []
+        y_window = w1_raw + w2_raw
+        y_bank = []
         for t in range(TILES):
-            yb = psum.tile([P, S], F32, name="y_bank%d" % t, tag="bank%d" % (2 * t))
-            ys = keep.tile([P, S], F32, name="y_sb%d" % t, tag="y_sb%d" % t, align_bytes=64)
-            product(yb[:], w1_codes, w1_scales, t, xq_words, xq_scales, whole)
-            nc.scalar.copy(ys[:], yb[:])
+            bank = psum.tile([P, S], F32, name="y_bank%d" % t, tag="bank%d" % (2 * t))
+            product(bank[:], w1_codes, w1_scales, t, xq_words, xq_scales, whole)
+            nc.scalar.copy(y_window[t][:, :S], bank[:])
             if t == 0:
-                round_weights(w2_grouped, w2_raw, 1, 0, P // 2, True)
-            y_bank.append(yb)
-            y_sb.append(ys)
-        y_far = [keep.tile([P, S], F32, name="y_far%d" % t) for t in range(TILES)]
+                round_on_scalar(w2_grouped, w2_raw, 1, 0, P // 2)
+            y_bank.append(bank)
+        d_window = [keep.tile([P, 2 * S], F32, name="d_window%d" % t) for t in range(TILES)]
+        y_far = [d_window[t][:, S:] for t in range(TILES)]
 
         def fetch_y(t):
-            for cols in halves:
-                nc.vector.tensor_copy(y_far[t][:, cols], y_sb[t][:].indirect(n1_sb[:, cols.start // 16 : cols.stop // 16]))
+            nc.vector.tensor_copy(y_far[t], y_window[t][:].indirect(n1_sb[:]))
 
         fetch_y(0)
-        w2_codes, w2_scales = planes("w2", "y_sb0")
-        quantize(w2_codes, w2_scales, w2_grouped, 0, H)
+        w2_codes, w2_scales = mx_operand("w2", "w1_raw0")
+        quantize_weights(w2_codes, w2_scales, w2_grouped)
         for t in range(1, TILES):
             fetch_y(t)
+        d_bank = []
         for t in range(TILES):
-            db = psum.tile([P, S], F32, name="d_bank%d" % t, tag="bank%d" % (2 * t + 1))
-            product(db[:], w2_codes, w2_scales, t, two_words, two_scales, whole)
-            ds = keep.tile([P, S], F32, name="d_sb%d" % t)
-            nc.scalar.copy(ds[:], db[:])
-            d_bank.append(db)
-            d_sb.append(ds)
+            bank = psum.tile([P, S], F32, name="d_bank%d" % t, tag="bank%d" % (2 * t + 1))
+            product(bank[:], w2_codes, w2_scales, t, two_words, two_scales, whole)
+            nc.scalar.copy(d_window[t][:, :S], bank[:])
+            d_bank.append(bank)
 
-        s_sb = [keep.tile([P, 2 * S], F32, name="s_sb%d" % t) for t in range(TILES)]
-        z_codes, z_scales = planes("z", "z_codes")
-        z_grouped = keep.tile([P, S * PACK], BF16, name="z_grouped", align_bytes=64)
+        s_window = [keep.tile([P, 2 * S], F32, name="s_window%d" % t) for t in range(TILES)]
+        z_codes, z_scales = mx_operand("z", "z_codes")
+        z_grouped = keep.tile([P, S * PACK], BF16, name="z_grouped", align_bytes=MX_ALIGN)
         z_slots = z_grouped[:].rearrange("p (c t) -> p c t", t=PACK)
 
-        excess = keep.tile([P, S], F32, name="excess")
-        nc.gpsimd.tensor_tensor(excess[:], d_sb[0][:], y_far[0][:], ALU.subtract)
-        clipped = keep.tile([P, S], F32, name="clipped")
-        nc.scalar.activation(clipped[:], excess[:], RELU)
-        smaller0 = keep.tile([P, S], F32, name="smaller0")
-        nc.gpsimd.tensor_tensor(smaller0[:], d_sb[0][:], clipped[:], ALU.subtract)
+        clipped = []
+        for t in range(RELU_TILES):
+            excess = keep.tile([P, S], F32, name="excess%d" % t)
+            nc.gpsimd.tensor_tensor(excess[:], d_window[t][:, :S], y_far[t], ALU.subtract)
+            clipped.append(keep.tile([P, S], F32, name="clipped%d" % t))
+            nc.scalar.activation(clipped[t][:], excess[:], RELU)
 
-        def spread_piece(t, first, count):
-            cols = slice(first, first + count)
-            entries = slice(first // 16, (first + count) // 16)
-            name = "%d_%d" % (t, first)
-            d_far = ring.tile([P, count], F32, name="d_far" + name, tag="fetched", align_bytes=64)
-            nc.vector.tensor_copy(d_far[:], d_sb[t][:].indirect(n2_sb[:, entries]))
-            if t == 0:
-                smaller = smaller0[:, cols]
-            else:
-                piece = keep.tile([P, count], F32, name="smaller" + name)
-                smaller = piece[:]
-                nc.vector.tensor_tensor(smaller, y_far[t][:, cols], d_bank[t][:, cols], ALU.min)
-            larger = s_sb[t][:, S + first : S + first + count]
-            nc.vector.tensor_tensor(larger, d_far[:], y_bank[t][:, cols], ALU.max)
-            spread = keep.tile([P, count], F32, name="spread" + name)
+        def minimum_by_relu(t):
+            smaller = keep.tile([P, S], F32, name="smaller%d" % t)
+            nc.gpsimd.tensor_tensor(smaller[:], d_window[t][:, :S], clipped[t][:], ALU.subtract)
+            return [smaller[:, cols] for cols in halves]
+
+        def minimum_on_vector(t, cols):
+            smaller = keep.tile([P, cols.stop - cols.start], F32, name="smaller%d_%d" % (t, cols.start))
+            nc.vector.tensor_tensor(smaller[:], y_far[t][:, cols], d_bank[t][:, cols], ALU.min)
+            return smaller[:]
+
+        def fetch_d(t, cols):
+            d_far = ring.tile([P, cols.stop - cols.start], F32, name="d_far%d_%d" % (t, cols.start), tag="fetched", align_bytes=MX_ALIGN)
+            nc.vector.tensor_copy(d_far[:], d_window[t][:].indirect(entries(n2_sb, cols)))
+            return d_far
+
+        def finish_z(t, cols, d_far, smaller):
+            larger = s_window[t][:, S + cols.start : S + cols.stop]
+            nc.vector.tensor_tensor(larger, d_far, y_bank[t][:, cols], ALU.max)
+            spread = keep.tile([P, cols.stop - cols.start], F32, name="spread%d_%d" % (t, cols.start))
             nc.gpsimd.tensor_tensor(spread[:], larger, smaller, ALU.subtract)
             nc.scalar.activation(z_slots[:, cols, t], spread[:], COPY, scale=gs_sb[:, t : t + 1])
 
-        for t in (1, 0, 2):
-            spread_piece(t, 0, HALF)
-            spread_piece(t, HALF, HALF)
-        spread_piece(3, 0, HALF)
-        spread_piece(3, HALF, P)
-        spread_piece(3, HALF + P, P)
-        cand_words = ring.tile([P, C], U32, name="cand_words", tag="fetched", align_bytes=64)
-        nc.vector.tensor_copy(cand_words[:].rearrange("p (t a b) -> p a t b", t=TILES, b=RUN), table_words[:].indirect(cand_sb[:]))
-        quantize(z_codes, z_scales, z_grouped, 0, HALF)
-        quantize(z_codes, z_scales, z_grouped, HALF, HALF)
+        last = TILES - 1
+        for t in range(last):
+            by_relu = minimum_by_relu(t) if t < RELU_TILES else None
+            d_far = fetch_d(t, whole)
+            for h, cols in enumerate(halves):
+                finish_z(t, cols, d_far[:, cols], by_relu[h] if by_relu else minimum_on_vector(t, cols))
+        d_far = fetch_d(last, halves[0])
+        finish_z(last, halves[0], d_far[:], minimum_on_vector(last, halves[0]))
+        d_far = fetch_d(last, halves[1])
+        for first in range(0, HALF, P):
+            cols = slice(HALF + first, HALF + first + P)
+            finish_z(last, cols, d_far[:, first : first + P], minimum_on_vector(last, cols))
 
-        bank = 0
-        for t in range(TILES):
-            for cols in halves if t == 0 else [whole]:
-                s_bank = psum.tile([P, cols.stop - cols.start], F32, name="s_bank%d" % bank, tag="bank%d" % bank)
-                product(s_bank[:], cand_words, cand_scales, t, z_codes, z_scales, cols)
-                nc.scalar.activation(s_sb[t][:, cols], s_bank[:], COPY, scale=0.0625)
-                bank = bank + 1
+        cand_words = ring.tile([P, C], U32, name="cand_words", tag="fetched", align_bytes=MX_ALIGN)
+        nc.vector.tensor_copy(cand_words[:].rearrange("p (t a b) -> p a t b", t=TILES, b=RUN), table_words[:].indirect(cand_sb[:]))
+        for cols in halves:
+            quantize(z_codes, z_scales, z_grouped, cols.start, HALF)
+
+        pieces = [(0, cols) for cols in halves] + [(t, whole) for t in range(1, TILES)]
+        for number, (t, cols) in enumerate(pieces):
+            bank = psum.tile([P, cols.stop - cols.start], F32, name="s_bank%d" % number, tag="bank%d" % number)
+            product(bank[:], cand_words, cand_scales, t, z_codes, z_scales, cols)
+            nc.scalar.activation(s_window[t][:, cols], bank[:], COPY, scale=0.0625)
 
         out_rows = out.rearrange("(a t b) n -> t a b n", t=TILES, b=RUN)
-        for t in range(TILES):
-            for cols in halves if t == TILES - 1 else [whole]:
-                count = cols.stop - cols.start
-                entries = slice(cols.start // 16, cols.stop // 16)
-                name = "%d_%d" % (t, cols.start)
-                far4 = keep.tile([P, count], F32, name="far4_" + name)
-                nc.vector.tensor_scalar(far4[:], s_sb[t][:].indirect(n4_sb[:, entries]), 0.75, 0.0, ALU.mult, ALU.add)
-                result = keep.tile([P, count], F32, name="result" + name)
-                if t < TILES - 1 or cols.start == 0:
-                    far3 = keep.tile([P, count], F32, name="far3_" + name)
-                    nc.vector.tensor_copy(far3[:], s_sb[t][:].indirect(n3_sb[:, entries]))
-                    nc.gpsimd.tensor_tensor(result[:], far3[:], far4[:], ALU.add)
-                else:
-                    nc.vector.tensor_tensor(result[:], s_sb[t][:].indirect(n3_sb[:, entries]), far4[:], ALU.add)
-                nc.sync.dma_start(out_rows[t][:, :, cols], result[:])
+        pieces = [(t, whole) for t in range(last)] + [(last, cols) for cols in halves]
+        for number, (t, cols) in enumerate(pieces):
+            count = cols.stop - cols.start
+            far4 = keep.tile([P, count], F32, name="far4_%d" % number)
+            nc.vector.tensor_scalar(far4[:], s_window[t][:].indirect(entries(n4_sb, cols)), 0.75, 0.0, ALU.mult, ALU.add)
+            result = keep.tile([P, count], F32, name="result%d" % number)
+            at_n3 = s_window[t][:].indirect(entries(n3_sb, cols))
+            if number < len(pieces) - 1:
+                far3 = keep.tile([P, count], F32, name="far3_%d" % number)
+                nc.vector.tensor_copy(far3[:], at_n3)
+                nc.gpsimd.tensor_tensor(result[:], far3[:], far4[:], ALU.add)
+            else:
+                nc.vector.tensor_tensor(result[:], at_n3, far4[:], ALU.add)
+            nc.sync.dma_start(out_rows[t][:, :, cols], result[:])

from contextlib import ExitStack

import concourse.mybir as mybir

K, T, S, H, C = 512, 2048, 512, 512, 512
FLOPS = 2 * K * H * S * 2 + 2 * H * C * S

F32 = mybir.dt.float32
BF16 = mybir.dt.bfloat16
I32 = mybir.dt.int32
U32 = mybir.dt.uint32
U16 = mybir.dt.uint16
U8 = mybir.dt.uint8
FP8X4 = mybir.dt.float8_e4m3fn_x4
ALU = mybir.AluOpType
COPY = mybir.ActivationFunctionType.Copy
RELU = mybir.ActivationFunctionType.Relu

P = 128
PACK = 4
TILES = 4
HALF = S // 2
GROUP = 16
RUN = 8
RELU_TILES = 2
MX_ALIGN = 64


def tile_picked_twcmaxbsum_none_p_kernel(tc, x_words, x_scales, w1, w2, gs, offs, two, n1, n2, cand, n3, n4, out):
    nc = tc.nc
    halves = [slice(0, HALF), slice(HALF, S)]
    whole = slice(0, S)

    with ExitStack() as ctx:
        lists = ctx.enter_context(tc.tile_pool(name="lists", bufs=1))
        keep = ctx.enter_context(tc.tile_pool(name="keep", bufs=1))
        ring = ctx.enter_context(tc.tile_pool(name="ring", bufs=2))
        psum = ctx.enter_context(tc.psum_pool(name="psum", bufs=1))

        def load_list(src, name):
            tile = lists.tile([P, S // GROUP], U16, name=name)
            nc.sync.dma_start(tile[:], src)
            return tile

        def entries(list_sb, cols):
            return list_sb[:, cols.start // GROUP : cols.stop // GROUP]

        def load_weights(w, name):
            parts = []
            for half in range(2):
                part = keep.tile([P, PACK * H // 2], F32, name="%s%d" % (name, half), tag="%s%d" % (name, half), align_bytes=MX_ALIGN)
                nc.sync.dma_start(
                    part[:].rearrange("p (j c) -> p j c", j=PACK),
                    w.rearrange("(p j) c -> p j c", j=PACK)[:, :, half * (H // 2) : (half + 1) * (H // 2)],
                )
                parts.append(part)
            return parts

        table_scales = keep.tile([P, T], U8, name="table_scales", align_bytes=MX_ALIGN)
        nc.vector.memset(table_scales[:].bitcast(I32), 0)
        offs_sb = load_list(offs, "offs_sb")
        for r in range(4):
            queue = nc.sync if r % 2 == 0 else nc.scalar
            queue.dma_start(table_scales[r:P:32, :].bitcast(I32), x_scales[0, r:16:4, :].bitcast(I32))
        two_sb = load_list(two, "two_sb")
        cand_sb = load_list(cand, "cand_sb")
        table_words = keep.tile([P, T], U32, name="table_words", align_bytes=MX_ALIGN)
        nc.sync.dma_start(table_words[:].bitcast(I32), x_words[0].rearrange("p n t -> p (n t)").bitcast(I32))
        w1_raw = load_weights(w1, "w1_raw")
        w2_raw = load_weights(w2, "w2_raw")
        n1_sb = load_list(n1, "n1_sb")
        n2_sb = load_list(n2, "n2_sb")
        gs_sb = keep.tile([P, TILES], F32, name="gs_sb")
        nc.sync.dma_start(gs_sb[:], gs.rearrange("(p t) o -> p (t o)", t=TILES))
        n4_sb = load_list(n4, "n4_sb")
        n3_sb = load_list(n3, "n3_sb")

        def gather_scales(list_sb, name):
            picked = keep.tile([P, S], U8, name=name, tag=name, align_bytes=MX_ALIGN)
            nc.vector.tensor_copy(picked[:], table_scales[:].indirect(list_sb[:]))
            return picked

        def gather_words(list_sb, name, tag):
            picked = keep.tile([P, S], U32, name=name, tag=tag, align_bytes=MX_ALIGN)
            nc.vector.tensor_copy(picked[:], table_words[:].indirect(list_sb[:]))
            return picked

        def dealt_views(grouped, raw, half, first, count):
            start = half * (P // 2) + first
            dealt = grouped[:].rearrange("p (t m j) -> p m j t", t=TILES, j=PACK)[:, start : start + count]
            rows = raw[half][:].rearrange("p (j m t) -> p m j t", j=PACK, t=TILES)[:, first : first + count]
            return dealt, rows

        def round_on_scalar(*piece):
            nc.scalar.activation(*dealt_views(*piece), COPY)

        def round_on_vector(*piece):
            nc.vector.tensor_copy(*dealt_views(*piece))

        def mx_operand(name, tag):
            codes = keep.tile([P, S], U32, name=name + "_codes", tag=tag, align_bytes=MX_ALIGN)
            scales = keep.tile([P, S], U8, name=name + "_scales", align_bytes=MX_ALIGN)
            return codes, scales

        def quantize(codes, scales, grouped, first, count):
            nc.vector.quantize_mx(
                out=codes[:, first : first + count].bitcast(FP8X4),
                scales=scales[:, first : first + count],
                in_=grouped[:, PACK * first : PACK * (first + count)],
            )

        def quantize_weights(codes, scales, grouped):
            for first, count in ((0, P), (P, P), (2 * P, 2 * P)):
                quantize(codes, scales, grouped, first, count)

        def product(bank, left, left_scales, t, right, right_scales, cols):
            rows = slice(t * P, (t + 1) * P)
            nc.tensor.matmul_mx(
                out=bank,
                lhsT=left[:, rows].bitcast(FP8X4),
                lhsT_scale=left_scales[:, rows],
                rhs=right[:, cols].bitcast(FP8X4),
                rhs_scale=right_scales[:, cols],
                start=True,
                stop=True,
            )

        xq_scales = gather_scales(offs_sb, "xq_scales")
        two_scales = gather_scales(two_sb, "two_scales")
        cand_listed = gather_scales(cand_sb, "cand_listed")
        xq_words = gather_words(offs_sb, "xq_words", "xq_words")
        w1_grouped = keep.tile([P, H * PACK], BF16, name="w1_grouped", tag="w1_grouped", align_bytes=MX_ALIGN)
        round_on_scalar(w1_grouped, w1_raw, 0, 0, P // 2)
        round_on_scalar(w1_grouped, w1_raw, 1, 0, P // 4)
        round_on_vector(w1_grouped, w1_raw, 1, P // 4, P // 4)
        w1_codes, w1_scales = mx_operand("w1", "w1_codes")
        quantize_weights(w1_codes, w1_scales, w1_grouped)

        cand_scales = keep.tile([P, C], U8, name="cand_scales", tag="w1_grouped", align_bytes=MX_ALIGN)
        nc.vector.tensor_copy(
            cand_scales[:].bitcast(I32).rearrange("p (t a b) -> p t a b", t=TILES, b=RUN // 4),
            cand_listed[:].bitcast(I32).rearrange("p (a t b) -> p t a b", t=TILES, b=RUN // 4),
        )
        two_words = gather_words(two_sb, "two_words", "cand_listed")
        w2_grouped = keep.tile([P, H * PACK], BF16, name="w2_grouped", align_bytes=MX_ALIGN)
        round_on_scalar(w2_grouped, w2_raw, 0, 0, P // 2)

        y_window = w1_raw + w2_raw
        y_bank = []
        for t in range(TILES):
            bank = psum.tile([P, S], F32, name="y_bank%d" % t, tag="bank%d" % (2 * t))
            product(bank[:], w1_codes, w1_scales, t, xq_words, xq_scales, whole)
            nc.scalar.copy(y_window[t][:, :S], bank[:])
            if t == 0:
                round_on_scalar(w2_grouped, w2_raw, 1, 0, P // 2)
            y_bank.append(bank)
        d_window = [keep.tile([P, 2 * S], F32, name="d_window%d" % t) for t in range(TILES)]
        y_far = [d_window[t][:, S:] for t in range(TILES)]

        def fetch_y(t):
            nc.vector.tensor_copy(y_far[t], y_window[t][:].indirect(n1_sb[:]))

        fetch_y(0)
        w2_codes, w2_scales = mx_operand("w2", "w1_raw0")
        quantize_weights(w2_codes, w2_scales, w2_grouped)
        for t in range(1, TILES):
            fetch_y(t)
        d_bank = []
        for t in range(TILES):
            bank = psum.tile([P, S], F32, name="d_bank%d" % t, tag="bank%d" % (2 * t + 1))
            product(bank[:], w2_codes, w2_scales, t, two_words, two_scales, whole)
            nc.scalar.copy(d_window[t][:, :S], bank[:])
            d_bank.append(bank)

        s_window = [keep.tile([P, 2 * S], F32, name="s_window%d" % t) for t in range(TILES)]
        z_codes, z_scales = mx_operand("z", "z_codes")
        z_grouped = keep.tile([P, S * PACK], BF16, name="z_grouped", align_bytes=MX_ALIGN)
        z_slots = z_grouped[:].rearrange("p (c t) -> p c t", t=PACK)

        clipped = []
        for t in range(RELU_TILES):
            excess = keep.tile([P, S], F32, name="excess%d" % t)
            nc.gpsimd.tensor_tensor(excess[:], d_window[t][:, :S], y_far[t], ALU.subtract)
            clipped.append(keep.tile([P, S], F32, name="clipped%d" % t))
            nc.scalar.activation(clipped[t][:], excess[:], RELU)

        def minimum_by_relu(t):
            smaller = keep.tile([P, S], F32, name="smaller%d" % t)
            nc.gpsimd.tensor_tensor(smaller[:], d_window[t][:, :S], clipped[t][:], ALU.subtract)
            return [smaller[:, cols] for cols in halves]

        def minimum_on_vector(t, cols):
            smaller = keep.tile([P, cols.stop - cols.start], F32, name="smaller%d_%d" % (t, cols.start))
            nc.vector.tensor_tensor(smaller[:], y_far[t][:, cols], d_bank[t][:, cols], ALU.min)
            return smaller[:]

        def fetch_d(t, cols):
            d_far = ring.tile([P, cols.stop - cols.start], F32, name="d_far%d_%d" % (t, cols.start), tag="fetched", align_bytes=MX_ALIGN)
            nc.vector.tensor_copy(d_far[:], d_window[t][:].indirect(entries(n2_sb, cols)))
            return d_far

        def finish_z(t, cols, d_far, smaller):
            larger = s_window[t][:, S + cols.start : S + cols.stop]
            nc.vector.tensor_tensor(larger, d_far, y_bank[t][:, cols], ALU.max)
            spread = keep.tile([P, cols.stop - cols.start], F32, name="spread%d_%d" % (t, cols.start))
            nc.gpsimd.tensor_tensor(spread[:], larger, smaller, ALU.subtract)
            nc.scalar.activation(z_slots[:, cols, t], spread[:], COPY, scale=gs_sb[:, t : t + 1])

        last = TILES - 1
        for t in range(last):
            by_relu = minimum_by_relu(t) if t < RELU_TILES else None
            d_far = fetch_d(t, whole)
            for h, cols in enumerate(halves):
                finish_z(t, cols, d_far[:, cols], by_relu[h] if by_relu else minimum_on_vector(t, cols))
        d_far = fetch_d(last, halves[0])
        finish_z(last, halves[0], d_far[:], minimum_on_vector(last, halves[0]))
        d_far = fetch_d(last, halves[1])
        for first in range(0, HALF, P):
            cols = slice(HALF + first, HALF + first + P)
            finish_z(last, cols, d_far[:, first : first + P], minimum_on_vector(last, cols))

        cand_words = ring.tile([P, C], U32, name="cand_words", tag="fetched", align_bytes=MX_ALIGN)
        nc.vector.tensor_copy(cand_words[:].rearrange("p (t a b) -> p a t b", t=TILES, b=RUN), table_words[:].indirect(cand_sb[:]))
        for cols in halves:
            quantize(z_codes, z_scales, z_grouped, cols.start, HALF)

        pieces = [(0, cols) for cols in halves] + [(t, whole) for t in range(1, TILES)]
        for number, (t, cols) in enumerate(pieces):
            bank = psum.tile([P, cols.stop - cols.start], F32, name="s_bank%d" % number, tag="bank%d" % number)
            product(bank[:], cand_words, cand_scales, t, z_codes, z_scales, cols)
            nc.scalar.activation(s_window[t][:, cols], bank[:], COPY, scale=0.0625)

        out_rows = out.rearrange("(a t b) n -> t a b n", t=TILES, b=RUN)
        pieces = [(t, whole) for t in range(last)] + [(last, cols) for cols in halves]
        for number, (t, cols) in enumerate(pieces):
            count = cols.stop - cols.start
            far4 = keep.tile([P, count], F32, name="far4_%d" % number)
            nc.vector.tensor_scalar(far4[:], s_window[t][:].indirect(entries(n4_sb, cols)), 0.75, 0.0, ALU.mult, ALU.add)
            result = keep.tile([P, count], F32, name="result%d" % number)
            at_n3 = s_window[t][:].indirect(entries(n3_sb, cols))
            if number < len(pieces) - 1:
                far3 = keep.tile([P, count], F32, name="far3_%d" % number)
                nc.vector.tensor_copy(far3[:], at_n3)
                nc.gpsimd.tensor_tensor(result[:], far3[:], far4[:], ALU.add)
            else:
                nc.vector.tensor_tensor(result[:], at_n3, far4[:], ALU.add)
            nc.sync.dma_start(out_rows[t][:, :, cols], result[:])
